import numpy as np, ml_dtypes
CORES = [33,38,57,62,81,86,161,166,185,190,209,214]
N = 12
GR, GC = 3, 4
L, KA, KB, F = 12, 3, 4, 32
def setup_inputs(rng):
    return {"a": rng.standard_normal((N, 128, KA * 128), dtype=np.float32).astype(ml_dtypes.bfloat16), "b": rng.standard_normal((N, 128, KB * F), dtype=np.float32).astype(ml_dtypes.bfloat16)}
def reference(a, b):
    A, B = a.astype(np.float64), b.astype(np.float64)
    y = np.zeros((N, 128, F))
    for i in range(GR):
        for j in range(GC):
            for k in range(L):
                At = A[i * GC + k // KA][:, 128 * (k % KA):128 * (k % KA) + 128]
                Bt = B[(k // KB) * GC + j][:, F * (k % KB):F * (k % KB) + F]
                y[i * GC + j] += At.T @ Bt
    return {"y": y.astype(ml_dtypes.bfloat16 if a.dtype != np.float64 else np.float64)}

@@ -1,0 +1,209 @@
+from concourse.bass import DstId, RemoteDMATransfer
+from concourse.mybir import AluOpType
+
+GR, GC = 3, 4
+L, KA, KB, F = 12, 3, 4, 32
+P = 128
+HK = 2 * KA
+
+SCRATCH = {
+    "bc4": ("sbuf", [P, 2, KB * F], "bfloat16"),
+    "bc2": ("sbuf", [P, 2, 2, 2 * F], "bfloat16"),
+    "bl4": ("sbuf", [P, 2, KB * F], "bfloat16"),
+    "bl2": ("sbuf", [P, 2, 2 * F], "bfloat16"),
+    "aa": ("sbuf", [P, HK * P], "bfloat16"),
+    "pout": ("sbuf", [P, 2 * F], "bfloat16"),
+    "pin": ("sbuf", [P, 2 * F], "bfloat16"),
+    "ysb": ("sbuf", [P, F], "bfloat16"),
+    "ps": ("psum", [P, 2 * F], "float32"),
+}
+SEMAPHORES = ["ldb", "lda", "xb", "xa", "r4", "r2", "mm", "cp", "rp", "ad", "st", "sent"]
+
+
+def _groups(r):
+    out = []
+    for t in range(KB):
+        m = (r * KB + t) // HK
+        if out and out[-1][0] == m:
+            out[-1][2] += 1
+        else:
+            out.append([m, t, 1])
+    return out
+
+
+def _bits(mask):
+    return [e for e in range(mask.bit_length()) if (mask >> e) & 1]
+
+
+def _split(mask, n):
+    b = _bits(mask)
+    w = len(b) // n
+    return [sum(1 << e for e in b[x * w:(x + 1) * w]) for x in range(n)]
+
+
+def _masks(topo, c, writes):
+    if not writes:
+        return []
+    ok = topo.mask(c, writes[0][2])
+    for w in writes:
+        ok &= topo.mask(c, w[2])
+    return _split(ok, len(writes))
+
+
+def _plan(T, topo):
+    cores = list(T.cores)
+    pair, near, far = {}, {}, {}
+    for i in range(GR):
+        for m in range(GC // 2):
+            pair[(i, m)] = [cores[i * GC + 2 * m], cores[i * GC + 2 * m + 1]]
+    for (i, m), p in pair.items():
+        assert (topo.host(p[0]), topo.chip(p[0])) == (topo.host(p[1]), topo.chip(p[1]))
+        able = [s for s in (0, 1) if all(topo.may_write(p[s], d) for d in pair[(i, 1 - m)])]
+        far[(i, m)] = able[-1]
+        near[(i, m)] = 1 - able[-1]
+    early = {c: [] for c in cores}
+    late = {c: [] for c in cores}
+    for (r, mj), p in pair.items():
+        order = [p[near[(r, mj)]], p[far[(r, mj)]]]
+        todo = {c: [] for c in p}
+        for gi, (m, _t0, nt) in enumerate(_groups(r)):
+            for i in range(GR):
+                if (i, m) == (r, mj):
+                    continue
+                role = near if m == mj else far
+                d = pair[(i, m)][role[(i, m)]]
+                todo[[c for c in order if topo.may_write(c, d)][0]].append((gi, nt, d))
+        for c in p:
+            lst = todo[c]
+            while len(lst) > 2:
+                single = [w for w in lst if sum(1 for v in lst if v[0] == w[0]) == 1]
+                w = (single or lst)[-1]
+                lst.remove(w)
+                for x in p:
+                    assert topo.may_write(x, w[2])
+                    early[x].append(w)
+            late[c] = lst
+    return pair, near, far, early, late
+
+
+def rank_program(g, core, T, topo):
+    rank = T.rank_of(core)
+    if rank is None:
+        return
+    S = T.sem
+    pair, near, far, early, late = _plan(T, topo)
+    i, j = rank // GC, rank % GC
+    m, s = j // 2, j % 2
+    me, other = (i, m), (i, 1 - m)
+    sib = pair[me][1 - s]
+    is_far = far[me] == s
+    grp = _groups(i)
+    whole = len(grp) == 1
+
+    def part(gi, x):
+        return T.bc4[:, x, :] if whole else T.bc2[:, gi, x, :]
+
+    def both(gi):
+        return T.bc4[:, :, :] if whole else T.bc2[:, gi, :, :]
+
+    def land(nt):
+        return (T.bl4, S.r4) if nt == KB else (T.bl2, S.r2)
+
+    def out_mask(c):
+        return sum(_masks(topo, c, late[c]))
+
+    def in_mask(c):
+        x = pair[me][0] if c != pair[me][0] else pair[me][1]
+        return topo.mask(c, x) & ~out_mask(c)
+
+    sent = [0]
+
+    def call(items):
+        trs = []
+        for d, mask, sem, src, dst in items:
+            rid, pid = topo.addr(d, core)
+            trs.append(RemoteDMATransfer(dst_ids=[DstId(rid=rid, pnc=pid)], dma_engine_mask=mask, remote_sem=sem,
+                                         src=src, dst=dst))
+            sent[0] += len(_bits(mask))
+        g.remote_dma_fused(trs, local_sem=S.sent)
+
+    need = {KB: 0, 2: 0}
+    for c in T.cores:
+        for lst in (early[c], late[c]):
+            for w, mask in zip(lst, _masks(topo, c, lst)):
+                if w[2] == core:
+                    need[w[1]] += len(_bits(mask))
+    n_xb = len(_bits(out_mask(sib)))
+    n_xa = len(_bits(in_mask(sib)))
+    pf = pair[other][far[other]]
+    n_rp = len(_bits(_masks(topo, pf, [(0, 0, d) for d in pair[me]])[s]))
+    if is_far:
+        n_rp += len(_bits(topo.mask(sib, core)))
+
+    own_a = T.aa[:, s * KA * P:(s + 1) * KA * P]
+    g.sync.dma_start(T.bc4[:, s, :] if whole else T.bc2[:, :, s, :], T.b[:, :]).then_inc(S.ldb, 16)
+    g.scalar.dma_start(own_a, T.a[:, :]).then_inc(S.lda, 16)
+
+    g.wait_ge(S.ldb, 16)
+    call([(sib, mask, S.xb, part(gi, s), part(gi, s)) for gi, mask in zip(range(len(grp)), _split(out_mask(core), len(grp)))])
+    if early[core]:
+        call([(d, mask, land(nt)[1], part(gi, s), land(nt)[0][:, s, :])
+              for (gi, nt, d), mask in zip(early[core], _masks(topo, core, early[core]))])
+    g.wait_ge(S.lda, 16)
+    call([(sib, in_mask(core), S.xa, own_a, own_a)])
+    g.wait_ge(S.xb, n_xb)
+    call([(d, mask, land(nt)[1], both(gi), land(nt)[0][:, :, :])
+          for (gi, nt, d), mask in zip(late[core], _masks(topo, core, late[core]))])
+    g.wait_ge(S.cp, 1)
+    if is_far:
+        q = pair[other]
+        call([(q[x], mask, S.rp, T.pout[:, x * F:(x + 1) * F], T.pin[:, F:2 * F])
+              for x, mask in zip((0, 1), _masks(topo, core, [(0, 0, d) for d in q]))])
+    else:
+        call([(sib, topo.mask(core, sib), S.rp, T.pout[:, 0:F], T.pin[:, 0:F])])
+    g.wait_ge(S.sent, sent[0])
+
+    src_half = other[1] if is_far else m
+    chunks = []
+    for r in range(GR):
+        for gi, (mm, t0, nt) in enumerate(_groups(r)):
+            if mm == m:
+                chunks.append(((r, src_half) != me, nt, r, gi, t0))
+    chunks.sort()
+    te = g.tensor
+    te.wait_ge(S.lda, 16)
+    te.wait_ge(S.xa, n_xa)
+    done = 0
+    for remote, nt, r, gi, t0 in chunks:
+        if remote:
+            te.wait_ge(land(nt)[1], need[nt])
+        else:
+            te.wait_ge(S.ldb, 16)
+            te.wait_ge(S.xb, n_xb)
+        for tt in range(nt):
+            cols = slice(tt * F, (tt + 1) * F)
+            if remote:
+                rhs = land(nt)[0][:, :, cols]
+            else:
+                rhs = T.bc4[:, :, cols] if whole else T.bc2[:, gi, :, cols]
+            ka = r * KB + t0 + tt - m * HK
+            done += 1
+            mmul = te.matmul(out=T.ps[:, :], lhsT=T.aa[:, ka * P:(ka + 1) * P], rhs=rhs, start=done == 1, stop=done == HK)
+    mmul.then_inc(S.mm, 1)
+
+    ve = g.vector
+    ve.wait_ge(S.mm, 1)
+    if is_far:
+        ve.tensor_copy(out=T.pout[:, :], in_=T.ps[:, :]).then_inc(S.cp, 1)
+        ve.wait_ge(S.rp, n_rp)
+        ve.tensor_tensor(out=T.ysb[:, :], in0=T.pin[:, 0:F], in1=T.pin[:, F:2 * F], op=AluOpType.add).then_inc(S.ad, 1)
+    else:
+        x = 1 - s
+        ve.tensor_copy(out=T.pout[:, 0:F], in_=T.ps[:, x * F:(x + 1) * F]).then_inc(S.cp, 1)
+        ve.wait_ge(S.rp, n_rp)
+        ve.tensor_tensor(out=T.ysb[:, :], in0=T.ps[:, s * F:(s + 1) * F], in1=T.pin[:, F:2 * F],
+                         op=AluOpType.add).then_inc(S.ad, 1)
+
+    g.sync.wait_ge(S.ad, 1)
+    g.sync.dma_start(T.y[:, :], T.ysb[:, :]).then_inc(S.st, 16)
+    g.sync.wait_ge(S.st, 16)

@@ -5,30 +5,19 @@ GR, GC = 3, 4
 L, KA, KB, F = 12, 3, 4, 32
 P = 128
 HK = 2 * KA
+WORLD = 256
 
 SCRATCH = {
-    "bc4": ("sbuf", [P, 2, KB * F], "bfloat16"),
-    "bc2": ("sbuf", [P, 2, 2, 2 * F], "bfloat16"),
-    "bl4": ("sbuf", [P, 2, KB * F], "bfloat16"),
-    "bl2": ("sbuf", [P, 2, 2 * F], "bfloat16"),
-    "aa": ("sbuf", [P, HK * P], "bfloat16"),
+    "aa": ("sbuf", [P, L * P], "bfloat16"),
+    "bb": ("sbuf", [P, GC, L * F], "bfloat16"),
     "pout": ("sbuf", [P, 2 * F], "bfloat16"),
-    "pin": ("sbuf", [P, 2 * F], "bfloat16"),
+    "pin": ("sbuf", [P, F], "bfloat16"),
     "ysb": ("sbuf", [P, F], "bfloat16"),
-    "ps": ("psum", [P, 2 * F], "float32"),
+    "psf": ("psum", [P, 512], "float32"),
+    "pso": ("psum", [P, 512], "float32"),
 }
-SEMAPHORES = ["ldb", "lda", "xb", "xa", "r4", "r2", "mm", "cp", "rp", "ad", "st", "sent"]
-
-
-def _groups(r):
-    out = []
-    for t in range(KB):
-        m = (r * KB + t) // HK
-        if out and out[-1][0] == m:
-            out[-1][2] += 1
-        else:
-            out.append([m, t, 1])
-    return out
+SEMAPHORES = ["ldb", "lda", "ae", "al", "bf", "be", "bl", "rb", "mf", "mo", "cp", "rp", "ad", "st", "sent"]
+FEED_B, FAR_B, FEED_A, SWAP_A, OWN_B, SHIP_A, PASS_B, PASS_A = range(8)
 
 
 def _bits(mask):
@@ -41,168 +30,178 @@ def _split(mask, n):
     return [sum(1 << e for e in b[x * w:(x + 1) * w]) for x in range(n)]
 
 
-def _masks(topo, c, writes):
-    if not writes:
-        return []
-    ok = topo.mask(c, writes[0][2])
-    for w in writes:
-        ok &= topo.mask(c, w[2])
-    return _split(ok, len(writes))
+def _on_chip(topo, a, b):
+    return (topo.host(a), topo.chip(a)) == (topo.host(b), topo.chip(b))
 
 
 def _plan(T, topo):
     cores = list(T.cores)
-    pair, near, far = {}, {}, {}
+
+    def rk(i, j):
+        return cores[i * GC + j]
+
+    def relay(c, d):
+        return [x for x in range(WORLD) if _on_chip(topo, x, c) and topo.die(x) == topo.die(c) and x not in cores
+                and topo.may_write(x, d)][0]
+
+    far = {}
     for i in range(GR):
         for m in range(GC // 2):
-            pair[(i, m)] = [cores[i * GC + 2 * m], cores[i * GC + 2 * m + 1]]
-    for (i, m), p in pair.items():
-        assert (topo.host(p[0]), topo.chip(p[0])) == (topo.host(p[1]), topo.chip(p[1]))
-        able = [s for s in (0, 1) if all(topo.may_write(p[s], d) for d in pair[(i, 1 - m)])]
-        far[(i, m)] = able[-1]
-        near[(i, m)] = 1 - able[-1]
-    early = {c: [] for c in cores}
-    late = {c: [] for c in cores}
-    for (r, mj), p in pair.items():
-        order = [p[near[(r, mj)]], p[far[(r, mj)]]]
-        todo = {c: [] for c in p}
-        for gi, (m, _t0, nt) in enumerate(_groups(r)):
-            for i in range(GR):
-                if (i, m) == (r, mj):
-                    continue
-                role = near if m == mj else far
-                d = pair[(i, m)][role[(i, m)]]
-                todo[[c for c in order if topo.may_write(c, d)][0]].append((gi, nt, d))
-        for c in p:
-            lst = todo[c]
-            while len(lst) > 2:
-                single = [w for w in lst if sum(1 for v in lst if v[0] == w[0]) == 1]
-                w = (single or lst)[-1]
-                lst.remove(w)
-                for x in p:
-                    assert topo.may_write(x, w[2])
-                    early[x].append(w)
-            late[c] = lst
-    return pair, near, far, early, late
+            p = [rk(i, 2 * m), rk(i, 2 * m + 1)]
+            q = [rk(i, 2 - 2 * m), rk(i, 3 - 2 * m)]
+            assert _on_chip(topo, p[0], p[1])
+            far[(i, m)] = [c for c in p if all(topo.may_write(c, d) for d in q)][-1]
+    terms = {c: [] for c in cores}
+    for i in range(GR):
+        for j in range(GC):
+            for k in range(L):
+                w = rk(i, j)
+                if k // HK != j // 2:
+                    f, hb = far[(i, k // HK)], rk(k // KB, j)
+                    if hb == f or topo.may_write(hb, f):
+                        w = f
+                terms[w].append((i, j, k))
+    items = set()
+    for w, lst in terms.items():
+        for i, j, k in lst:
+            hb, ha = rk(k // KB, j), rk(i, k // KA)
+            mine = w == rk(i, j)
+            if hb != w:
+                if topo.may_write(hb, w):
+                    items.add((OWN_B if mine else FAR_B, "B", hb, w, j, "be" if mine else "bf", k))
+                else:
+                    items.add((FEED_B, "B", hb, relay(hb, w), j, "rb", k))
+                    items.add((PASS_B, "B", relay(hb, w), w, j, "bl", k))
+            if ha != w:
+                if topo.may_write(ha, w):
+                    items.add((SWAP_A if _on_chip(topo, ha, w) else SHIP_A, "A", ha, w, 0, "ae", k))
+                else:
+                    items.add((FEED_A, "A", ha, relay(ha, w), 0, "ae", k))
+                    items.add((PASS_A, "A", relay(ha, w), w, 0, "al", k))
+    runs = {}
+    for pr, kind, src, dst, j, sem, k in items:
+        runs.setdefault((pr, kind, src, dst, j, sem), []).append(k)
+    trs = {}
+    for (pr, kind, src, dst, j, sem), ks in runs.items():
+        ks.sort()
+        assert ks == list(range(ks[0], ks[0] + len(ks)))
+        trs.setdefault((src, pr, kind, j, ks[0], len(ks), sem), []).append(dst)
+    sends = {}
+    for key in sorted(trs):
+        sends.setdefault(key[0], []).append(key[1:] + (sorted(trs[key]),))
+    return rk, far, terms, sends
+
+
+def _mask(topo, T, c, pr, dsts):
+    away = [x for x in T.cores if not _on_chip(topo, x, c) and topo.may_write(c, x)][0]
+    ok = topo.mask(c, dsts[0])
+    for d in dsts:
+        ok &= topo.mask(c, d)
+    return ok & ~topo.mask(c, away) if pr == SWAP_A else ok & topo.mask(c, away)
 
 
 def rank_program(g, core, T, topo):
-    rank = T.rank_of(core)
-    if rank is None:
-        return
     S = T.sem
-    pair, near, far, early, late = _plan(T, topo)
-    i, j = rank // GC, rank % GC
-    m, s = j // 2, j % 2
-    me, other = (i, m), (i, 1 - m)
-    sib = pair[me][1 - s]
-    is_far = far[me] == s
-    grp = _groups(i)
-    whole = len(grp) == 1
+    rk, far, terms, sends = _plan(T, topo)
+    if core not in sends:
+        return
+    rank = T.rank_of(core)
 
-    def part(gi, x):
-        return T.bc4[:, x, :] if whole else T.bc2[:, gi, x, :]
+    def a_ap(k0, nk):
+        return T.aa[:, k0 * P:(k0 + nk) * P]
 
-    def both(gi):
-        return T.bc4[:, :, :] if whole else T.bc2[:, gi, :, :]
+    def b_ap(jj, k0, nk):
+        return T.bb[:, jj, k0 * F:(k0 + nk) * F]
 
-    def land(nt):
-        return (T.bl4, S.r4) if nt == KB else (T.bl2, S.r2)
+    need = {}
+    for c in sends:
+        for pr, _kind, _j, _k0, _nk, sem, dsts in sends[c]:
+            if core in dsts:
+                need[sem] = need.get(sem, 0) + len(_bits(_mask(topo, T, c, pr, dsts)))
 
-    def out_mask(c):
-        return sum(_masks(topo, c, late[c]))
-
-    def in_mask(c):
-        x = pair[me][0] if c != pair[me][0] else pair[me][1]
-        return topo.mask(c, x) & ~out_mask(c)
+    if rank is not None:
+        i, j = rank // GC, rank % GC
+        m = j // 2
+        owners = [rk(i, 2 - 2 * m), rk(i, 3 - 2 * m)]
+        is_far = far[(i, m)] == core
+        g.sync.dma_start(b_ap(j, i * KB, KB), T.b[:, :]).then_inc(S.ldb, 16)
+        g.scalar.dma_start(a_ap(j * KA, KA), T.a[:, :]).then_inc(S.lda, 16)
 
     sent = [0]
 
     def call(items):
         trs = []
-        for d, mask, sem, src, dst in items:
-            rid, pid = topo.addr(d, core)
-            trs.append(RemoteDMATransfer(dst_ids=[DstId(rid=rid, pnc=pid)], dma_engine_mask=mask, remote_sem=sem,
-                                         src=src, dst=dst))
+        for dsts, mask, sem, src, dst in items:
+            ids = [DstId(rid=topo.addr(d, core)[0], pnc=topo.addr(d, core)[1]) for d in dsts]
+            trs.append(RemoteDMATransfer(dst_ids=ids, dma_engine_mask=mask, remote_sem=sem, srcs=[src],
+                                         dsts=[dst for _d in dsts]))
             sent[0] += len(_bits(mask))
         g.remote_dma_fused(trs, local_sem=S.sent)
 
-    need = {KB: 0, 2: 0}
-    for c in T.cores:
-        for lst in (early[c], late[c]):
-            for w, mask in zip(lst, _masks(topo, c, lst)):
-                if w[2] == core:
-                    need[w[1]] += len(_bits(mask))
-    n_xb = len(_bits(out_mask(sib)))
-    n_xa = len(_bits(in_mask(sib)))
-    pf = pair[other][far[other]]
-    n_rp = len(_bits(_masks(topo, pf, [(0, 0, d) for d in pair[me]])[s]))
+    gate = {FEED_B: ("ldb", 16), FAR_B: ("ldb", 16), OWN_B: ("ldb", 16),
+            FEED_A: ("lda", 16), SWAP_A: ("lda", 16), SHIP_A: ("lda", 16),
+            PASS_B: ("rb", need.get("rb", 0)), PASS_A: ("ae", need.get("ae", 0))}
+    waited = set()
+    todo = sends[core]
+    if gate[todo[0][0]][0] == "lda":
+        todo = [t for t in todo if gate[t[0]][0] == "ldb"] + [t for t in todo if gate[t[0]][0] != "ldb"]
+    for pr, kind, jj, k0, nk, sem, dsts in todo:
+        if gate[pr][0] not in waited:
+            waited.add(gate[pr][0])
+            g.wait_ge(S[gate[pr][0]], gate[pr][1])
+        ap = a_ap(k0, nk) if kind == "A" else b_ap(jj, k0, nk)
+        call([(dsts, _mask(topo, T, core, pr, dsts), S[sem], ap, ap)])
+    if rank is None:
+        g.wait_ge(S.sent, sent[0])
+        return
     if is_far:
-        n_rp += len(_bits(topo.mask(sib, core)))
-
-    own_a = T.aa[:, s * KA * P:(s + 1) * KA * P]
-    g.sync.dma_start(T.bc4[:, s, :] if whole else T.bc2[:, :, s, :], T.b[:, :]).then_inc(S.ldb, 16)
-    g.scalar.dma_start(own_a, T.a[:, :]).then_inc(S.lda, 16)
-
-    g.wait_ge(S.ldb, 16)
-    call([(sib, mask, S.xb, part(gi, s), part(gi, s)) for gi, mask in zip(range(len(grp)), _split(out_mask(core), len(grp)))])
-    if early[core]:
-        call([(d, mask, land(nt)[1], part(gi, s), land(nt)[0][:, s, :])
-              for (gi, nt, d), mask in zip(early[core], _masks(topo, core, early[core]))])
-    g.wait_ge(S.lda, 16)
-    call([(sib, in_mask(core), S.xa, own_a, own_a)])
-    g.wait_ge(S.xb, n_xb)
-    call([(d, mask, land(nt)[1], both(gi), land(nt)[0][:, :, :])
-          for (gi, nt, d), mask in zip(late[core], _masks(topo, core, late[core]))])
-    g.wait_ge(S.cp, 1)
-    if is_far:
-        q = pair[other]
-        call([(q[x], mask, S.rp, T.pout[:, x * F:(x + 1) * F], T.pin[:, F:2 * F])
-              for x, mask in zip((0, 1), _masks(topo, core, [(0, 0, d) for d in q]))])
-    else:
-        call([(sib, topo.mask(core, sib), S.rp, T.pout[:, 0:F], T.pin[:, 0:F])])
+        g.wait_ge(S.cp, 1)
+        call([([owners[x]], mask, S.rp, T.pout[:, x * F:(x + 1) * F], T.pin[:, :])
+              for x, mask in zip((0, 1), _split(topo.mask(core, owners[0]) & topo.mask(core, owners[1]), 2))])
     g.wait_ge(S.sent, sent[0])
+    pf = far[(i, 1 - m)]
+    n_rp = len(_bits(_split(topo.mask(pf, rk(i, 2 * m)) & topo.mask(pf, rk(i, 2 * m + 1)), 2)[j % 2]))
 
-    src_half = other[1] if is_far else m
-    chunks = []
-    for r in range(GR):
-        for gi, (mm, t0, nt) in enumerate(_groups(r)):
-            if mm == m:
-                chunks.append(((r, src_half) != me, nt, r, gi, t0))
-    chunks.sort()
     te = g.tensor
-    te.wait_ge(S.lda, 16)
-    te.wait_ge(S.xa, n_xa)
-    done = 0
-    for remote, nt, r, gi, t0 in chunks:
-        if remote:
-            te.wait_ge(land(nt)[1], need[nt])
-        else:
-            te.wait_ge(S.ldb, 16)
-            te.wait_ge(S.xb, n_xb)
-        for tt in range(nt):
-            cols = slice(tt * F, (tt + 1) * F)
-            if remote:
-                rhs = land(nt)[0][:, :, cols]
-            else:
-                rhs = T.bc4[:, :, cols] if whole else T.bc2[:, gi, :, cols]
-            ka = r * KB + t0 + tt - m * HK
-            done += 1
-            mmul = te.matmul(out=T.ps[:, :], lhsT=T.aa[:, ka * P:(ka + 1) * P], rhs=rhs, start=done == 1, stop=done == HK)
-    mmul.then_inc(S.mm, 1)
+    seen = set()
+
+    def await_(names):
+        for n in names:
+            if n not in seen and (n in ("ldb", "lda") or need.get(n, 0)):
+                seen.add(n)
+                te.wait_ge(S[n], 16 if n in ("ldb", "lda") else need[n])
+
+    def group(lst, out, sem):
+        for x, (_i, jj, k) in enumerate(lst):
+            mmul = te.matmul(out=out, lhsT=a_ap(k, 1), rhs=b_ap(jj, k, 1), start=x == 0, stop=x == len(lst) - 1)
+        if sem is not None:
+            mmul.then_inc(sem, 1)
+
+    passed = set()
+    for c in sends:
+        for pr, kind, jj, k0, nk, _sem, dsts in sends[c]:
+            if core in dsts and pr in (PASS_B, PASS_A):
+                passed.update((kind, jj, k) for k in range(k0, k0 + nk))
+    mine = [t for t in terms[core] if t[1] == j]
+    if is_far:
+        await_(["ldb", "lda", "ae", "bf"])
+        cols = [[t for t in terms[core] if rk(t[0], t[1]) == o] for o in owners]
+        group(cols[0], T.psf[:, 0:F], None)
+        group(cols[1], T.psf[:, F:2 * F], S.mf)
+    soon = [t for t in mine if ("A", 0, t[2]) not in passed and ("B", t[1], t[2]) not in passed]
+    mine = soon + [t for t in mine if t not in soon]
+    for x, (_i, jj, k) in enumerate(mine):
+        await_(["ldb", "lda", "ae", "be"] if x < len(soon) else ["al", "bl"])
+        mmul = te.matmul(out=T.pso[:, 0:F], lhsT=a_ap(k, 1), rhs=b_ap(jj, k, 1), start=x == 0, stop=x == len(mine) - 1)
+    mmul.then_inc(S.mo, 1)
 
     ve = g.vector
-    ve.wait_ge(S.mm, 1)
     if is_far:
-        ve.tensor_copy(out=T.pout[:, :], in_=T.ps[:, :]).then_inc(S.cp, 1)
-        ve.wait_ge(S.rp, n_rp)
-        ve.tensor_tensor(out=T.ysb[:, :], in0=T.pin[:, 0:F], in1=T.pin[:, F:2 * F], op=AluOpType.add).then_inc(S.ad, 1)
-    else:
-        x = 1 - s
-        ve.tensor_copy(out=T.pout[:, 0:F], in_=T.ps[:, x * F:(x + 1) * F]).then_inc(S.cp, 1)
-        ve.wait_ge(S.rp, n_rp)
-        ve.tensor_tensor(out=T.ysb[:, :], in0=T.ps[:, s * F:(s + 1) * F], in1=T.pin[:, F:2 * F],
-                         op=AluOpType.add).then_inc(S.ad, 1)
+        ve.wait_ge(S.mf, 1)
+        ve.tensor_copy(out=T.pout[:, :], in_=T.psf[:, 0:2 * F]).then_inc(S.cp, 1)
+    ve.wait_ge(S.mo, 1)
+    ve.wait_ge(S.rp, n_rp)
+    ve.tensor_tensor(out=T.ysb[:, :], in0=T.pso[:, 0:F], in1=T.pin[:, :], op=AluOpType.add).then_inc(S.ad, 1)
 
     g.sync.wait_ge(S.ad, 1)
     g.sync.dma_start(T.y[:, :], T.ysb[:, :]).then_inc(S.st, 16)

from concourse.bass import DstId, RemoteDMATransfer
from concourse.mybir import AluOpType

GR, GC = 3, 4
L, KA, KB, F = 12, 3, 4, 32
P = 128
HK = 2 * KA
WORLD = 256

SCRATCH = {
    "aa": ("sbuf", [P, L * P], "bfloat16"),
    "bb": ("sbuf", [P, GC, L * F], "bfloat16"),
    "pout": ("sbuf", [P, 2 * F], "bfloat16"),
    "pin": ("sbuf", [P, F], "bfloat16"),
    "ysb": ("sbuf", [P, F], "bfloat16"),
    "psf": ("psum", [P, 512], "float32"),
    "pso": ("psum", [P, 512], "float32"),
}
SEMAPHORES = ["ldb", "lda", "ae", "al", "bf", "be", "bl", "rb", "mf", "mo", "cp", "rp", "ad", "st", "sent"]
FEED_B, FAR_B, FEED_A, SWAP_A, OWN_B, SHIP_A, PASS_B, PASS_A = range(8)


def _bits(mask):
    return [e for e in range(mask.bit_length()) if (mask >> e) & 1]


def _split(mask, n):
    b = _bits(mask)
    w = len(b) // n
    return [sum(1 << e for e in b[x * w:(x + 1) * w]) for x in range(n)]


def _on_chip(topo, a, b):
    return (topo.host(a), topo.chip(a)) == (topo.host(b), topo.chip(b))


def _plan(T, topo):
    cores = list(T.cores)

    def rk(i, j):
        return cores[i * GC + j]

    def relay(c, d):
        return [x for x in range(WORLD) if _on_chip(topo, x, c) and topo.die(x) == topo.die(c) and x not in cores
                and topo.may_write(x, d)][0]

    far = {}
    for i in range(GR):
        for m in range(GC // 2):
            p = [rk(i, 2 * m), rk(i, 2 * m + 1)]
            q = [rk(i, 2 - 2 * m), rk(i, 3 - 2 * m)]
            assert _on_chip(topo, p[0], p[1])
            far[(i, m)] = [c for c in p if all(topo.may_write(c, d) for d in q)][-1]
    terms = {c: [] for c in cores}
    for i in range(GR):
        for j in range(GC):
            for k in range(L):
                w = rk(i, j)
                if k // HK != j // 2:
                    f, hb = far[(i, k // HK)], rk(k // KB, j)
                    if hb == f or topo.may_write(hb, f):
                        w = f
                terms[w].append((i, j, k))
    items = set()
    for w, lst in terms.items():
        for i, j, k in lst:
            hb, ha = rk(k // KB, j), rk(i, k // KA)
            mine = w == rk(i, j)
            if hb != w:
                if topo.may_write(hb, w):
                    items.add((OWN_B if mine else FAR_B, "B", hb, w, j, "be" if mine else "bf", k))
                else:
                    items.add((FEED_B, "B", hb, relay(hb, w), j, "rb", k))
                    items.add((PASS_B, "B", relay(hb, w), w, j, "bl", k))
            if ha != w:
                if topo.may_write(ha, w):
                    items.add((SWAP_A if _on_chip(topo, ha, w) else SHIP_A, "A", ha, w, 0, "ae", k))
                else:
                    items.add((FEED_A, "A", ha, relay(ha, w), 0, "ae", k))
                    items.add((PASS_A, "A", relay(ha, w), w, 0, "al", k))
    runs = {}
    for pr, kind, src, dst, j, sem, k in items:
        runs.setdefault((pr, kind, src, dst, j, sem), []).append(k)
    trs = {}
    for (pr, kind, src, dst, j, sem), ks in runs.items():
        ks.sort()
        assert ks == list(range(ks[0], ks[0] + len(ks)))
        trs.setdefault((src, pr, kind, j, ks[0], len(ks), sem), []).append(dst)
    sends = {}
    for key in sorted(trs):
        sends.setdefault(key[0], []).append(key[1:] + (sorted(trs[key]),))
    return rk, far, terms, sends


def _mask(topo, T, c, pr, dsts):
    away = [x for x in T.cores if not _on_chip(topo, x, c) and topo.may_write(c, x)][0]
    ok = topo.mask(c, dsts[0])
    for d in dsts:
        ok &= topo.mask(c, d)
    return ok & ~topo.mask(c, away) if pr == SWAP_A else ok & topo.mask(c, away)


def rank_program(g, core, T, topo):
    S = T.sem
    rk, far, terms, sends = _plan(T, topo)
    if core not in sends:
        return
    rank = T.rank_of(core)

    def a_ap(k0, nk):
        return T.aa[:, k0 * P:(k0 + nk) * P]

    def b_ap(jj, k0, nk):
        return T.bb[:, jj, k0 * F:(k0 + nk) * F]

    need = {}
    for c in sends:
        for pr, _kind, _j, _k0, _nk, sem, dsts in sends[c]:
            if core in dsts:
                need[sem] = need.get(sem, 0) + len(_bits(_mask(topo, T, c, pr, dsts)))

    if rank is not None:
        i, j = rank // GC, rank % GC
        m = j // 2
        owners = [rk(i, 2 - 2 * m), rk(i, 3 - 2 * m)]
        is_far = far[(i, m)] == core
        g.sync.dma_start(b_ap(j, i * KB, KB), T.b[:, :]).then_inc(S.ldb, 16)
        g.scalar.dma_start(a_ap(j * KA, KA), T.a[:, :]).then_inc(S.lda, 16)

    sent = [0]

    def call(items):
        trs = []
        for dsts, mask, sem, src, dst in items:
            ids = [DstId(rid=topo.addr(d, core)[0], pnc=topo.addr(d, core)[1]) for d in dsts]
            trs.append(RemoteDMATransfer(dst_ids=ids, dma_engine_mask=mask, remote_sem=sem, srcs=[src],
                                         dsts=[dst for _d in dsts]))
            sent[0] += len(_bits(mask))
        g.remote_dma_fused(trs, local_sem=S.sent)

    gate = {FEED_B: ("ldb", 16), FAR_B: ("ldb", 16), OWN_B: ("ldb", 16),
            FEED_A: ("lda", 16), SWAP_A: ("lda", 16), SHIP_A: ("lda", 16),
            PASS_B: ("rb", need.get("rb", 0)), PASS_A: ("ae", need.get("ae", 0))}
    waited = set()
    todo = sends[core]
    if gate[todo[0][0]][0] == "lda":
        todo = [t for t in todo if gate[t[0]][0] == "ldb"] + [t for t in todo if gate[t[0]][0] != "ldb"]
    for pr, kind, jj, k0, nk, sem, dsts in todo:
        if gate[pr][0] not in waited:
            waited.add(gate[pr][0])
            g.wait_ge(S[gate[pr][0]], gate[pr][1])
        ap = a_ap(k0, nk) if kind == "A" else b_ap(jj, k0, nk)
        call([(dsts, _mask(topo, T, core, pr, dsts), S[sem], ap, ap)])
    if rank is None:
        g.wait_ge(S.sent, sent[0])
        return
    if is_far:
        g.wait_ge(S.cp, 1)
        call([([owners[x]], mask, S.rp, T.pout[:, x * F:(x + 1) * F], T.pin[:, :])
              for x, mask in zip((0, 1), _split(topo.mask(core, owners[0]) & topo.mask(core, owners[1]), 2))])
    g.wait_ge(S.sent, sent[0])
    pf = far[(i, 1 - m)]
    n_rp = len(_bits(_split(topo.mask(pf, rk(i, 2 * m)) & topo.mask(pf, rk(i, 2 * m + 1)), 2)[j % 2]))

    te = g.tensor
    seen = set()

    def await_(names):
        for n in names:
            if n not in seen and (n in ("ldb", "lda") or need.get(n, 0)):
                seen.add(n)
                te.wait_ge(S[n], 16 if n in ("ldb", "lda") else need[n])

    def group(lst, out, sem):
        for x, (_i, jj, k) in enumerate(lst):
            mmul = te.matmul(out=out, lhsT=a_ap(k, 1), rhs=b_ap(jj, k, 1), start=x == 0, stop=x == len(lst) - 1)
        if sem is not None:
            mmul.then_inc(sem, 1)

    passed = set()
    for c in sends:
        for pr, kind, jj, k0, nk, _sem, dsts in sends[c]:
            if core in dsts and pr in (PASS_B, PASS_A):
                passed.update((kind, jj, k) for k in range(k0, k0 + nk))
    mine = [t for t in terms[core] if t[1] == j]
    if is_far:
        await_(["ldb", "lda", "ae", "bf"])
        cols = [[t for t in terms[core] if rk(t[0], t[1]) == o] for o in owners]
        group(cols[0], T.psf[:, 0:F], None)
        group(cols[1], T.psf[:, F:2 * F], S.mf)
    soon = [t for t in mine if ("A", 0, t[2]) not in passed and ("B", t[1], t[2]) not in passed]
    mine = soon + [t for t in mine if t not in soon]
    for x, (_i, jj, k) in enumerate(mine):
        await_(["ldb", "lda", "ae", "be"] if x < len(soon) else ["al", "bl"])
        mmul = te.matmul(out=T.pso[:, 0:F], lhsT=a_ap(k, 1), rhs=b_ap(jj, k, 1), start=x == 0, stop=x == len(mine) - 1)
    mmul.then_inc(S.mo, 1)

    ve = g.vector
    if is_far:
        ve.wait_ge(S.mf, 1)
        ve.tensor_copy(out=T.pout[:, :], in_=T.psf[:, 0:2 * F]).then_inc(S.cp, 1)
    ve.wait_ge(S.mo, 1)
    ve.wait_ge(S.rp, n_rp)
    ve.tensor_tensor(out=T.ysb[:, :], in0=T.pso[:, 0:F], in1=T.pin[:, :], op=AluOpType.add).then_inc(S.ad, 1)

    g.sync.wait_ge(S.ad, 1)
    g.sync.dma_start(T.y[:, :], T.ysb[:, :]).then_inc(S.st, 16)
    g.sync.wait_ge(S.st, 16)
